import numpy as np
import ml_dtypes


def mxq(x, axis, fmt="e4m3"):
    dtype, down = {"e4m3": (ml_dtypes.float8_e4m3fn, 7), "e5m2": (ml_dtypes.float8_e5m2, 14)}[fmt]
    v = np.moveaxis(np.asarray(x, np.float32).astype(ml_dtypes.bfloat16).astype(np.float64), axis, -1)
    blocks = v.reshape(v.shape[:-1] + (-1, 32))
    amax = np.abs(blocks).max(-1, keepdims=True)
    byte = np.maximum(np.where(amax > 0, np.frexp(amax)[1] - 1 + 127, 0) - down, 1)
    scale = np.exp2(byte - 127.0)
    codes = (blocks / scale).astype(np.float32).astype(dtype).astype(np.float64)
    return np.moveaxis((codes * scale).reshape(v.shape), -1, axis)


WIDE = False


def mx_kscale(k):
    if not WIDE:
        return np.ones(k)
    levels = np.array([10, -10, 5, -5, 0])
    if k % 512:
        return np.exp2(np.random.permutation(np.resize(levels, k // 32))).repeat(32)
    a = np.empty((k // 512, 16))
    for p in range(k // 512):
        a[p, :8] = np.random.permutation(np.resize(levels, 8))
        for g in range(8):
            far = levels[np.abs(levels - a[p, g]) >= 10]
            a[p, g + 8] = far[np.random.randint(len(far))]
    return np.exp2(a.ravel()).repeat(32)


def f64(x):
    return np.asarray(x).astype(np.float64)


def striped(idx):
    return np.tile(np.asarray(idx).reshape(-1, 16).T, (8, 1)).astype(np.uint16)


def unstriped(offs):
    return offs[:16].T.reshape(-1).astype(np.int64)


E2M1 = np.array([0.0, 0.5, 1.0, 1.5, 2.0, 3.0, 4.0, 6.0, -0.0, -0.5, -1.0, -1.5, -2.0, -3.0, -4.0, -6.0])


def pack_weight(w, fmt):
    k, n = w.shape
    w = f64(np.asarray(w, np.float32).astype(ml_dtypes.bfloat16)).reshape(k // 32, 32, n)
    amax = np.abs(w).max(1)
    if fmt == "e4m3":
        byte = np.frexp(amax)[1] - 1 + 127 - 7
    else:
        mant, ex = np.frexp(amax / 6.0)
        byte = np.where(mant > 0.5, ex, ex - 1) + 127
    byte = np.clip(np.where(amax > 0, byte, 1), 1, 254)
    scaled = (w * np.exp2(127.0 - byte)[:, None, :]).reshape(k, n).astype(np.float32)
    by_word = np.ascontiguousarray(scaled.reshape(k // 512, 128, 4, n).transpose(0, 1, 3, 2))
    if fmt == "e4m3":
        words = by_word.astype(ml_dtypes.float8_e4m3fn).view(np.uint8)
    else:
        c = by_word.astype(ml_dtypes.float4_e2m1fn).view(np.uint8) & 0xF
        words = (c[..., 0::2] | (c[..., 1::2] << 4)).reshape(k // 512, 128, 2 * n)
    return np.ascontiguousarray(words), np.ascontiguousarray(byte.astype(np.uint8).reshape(k // 512, 16, n))


def unpack_weight(words, scales, fmt):
    g, _, n = scales.shape
    words = np.ascontiguousarray(words).reshape(g, 128, n, -1)
    if fmt == "e4m3":
        vals = words.view(ml_dtypes.float8_e4m3fn).astype(np.float64)
    else:
        nib = np.empty((g, 128, n, 4), np.uint8)
        nib[..., 0::2] = words & 0xF
        nib[..., 1::2] = words >> 4
        vals = E2M1[nib]
    vals = vals * np.repeat(np.exp2(scales.astype(np.float64) - 127.0), 8, axis=1)[..., None]
    return vals.transpose(0, 1, 3, 2).reshape(g * 512, n)


B, N, T, D, NQ = 2, 512, 2048, 512, 128


def setup_inputs():
    n = np.random.standard_normal
    idx = np.random.permutation(T)[:B * N]
    s = mx_kscale(D)[:, None]
    kp = pack_weight(n((D, T)) / s, "e4m3")
    return {
        "qT": (n((B, D, NQ)) * s * (1.00 / np.sqrt(D))).astype(np.float32),
        "k_words": kp[0],
        "k_scales": kp[1],
        "offs": striped(idx),
    }


def reference(qT, k_words, k_scales, offs):
    idx = unstriped(offs)
    pick = lambda x, which: x[:, which].reshape(x.shape[0], B, -1).transpose(1, 0, 2)
    k = unpack_weight(k_words, k_scales, "e4m3")
    kg = pick(k, idx)
    qq = mxq(f64(qT), 1, "e4m3")
    a = qq.transpose(0, 2, 1) @ kg
    m = np.max(a, axis=-1, keepdims=True)
    e = np.exp(a - m)
    l = np.sum(e, axis=-1, keepdims=True)
    y = e / l
    out = np.zeros((B, NQ, T))
    for b in range(B):
        out[b][:, idx[b * N:(b + 1) * N]] = y[b]
    return out

@@ -1,0 +1,106 @@
+from contextlib import ExitStack
+
+import concourse.mybir as mybir
+
+B, N, T, D, NQ = 2, 512, 2048, 512, 128
+FLOPS = 2 * B * NQ * N * D
+
+F32 = mybir.dt.float32
+BF16 = mybir.dt.bfloat16
+I32 = mybir.dt.int32
+U32 = mybir.dt.uint32
+U16 = mybir.dt.uint16
+U8 = mybir.dt.uint8
+FP8X4 = mybir.dt.float8_e4m3fn_x4
+ACT = mybir.ActivationFunctionType
+ALU = mybir.AluOpType
+AXIS = mybir.AxisListType
+
+P = 128
+PACK = 4
+HALF = N // 2
+PER_COL = 16
+
+
+def tile_attend_wscat_topk_kernel(tc, qT, k_words, k_scales, offs, out):
+    nc = tc.nc
+    with ExitStack() as ctx:
+        keep = ctx.enter_context(tc.tile_pool(name="keep", bufs=1))
+        psum = ctx.enter_context(tc.psum_pool(name="psum", bufs=1))
+
+        offsets = keep.tile([P, B * N // PER_COL], U16, name="offsets")
+        pool_words = keep.tile([P, T], U32, name="pool_words", align_bytes=64)
+        pool_scales = keep.tile([P, T], U8, name="pool_scales", align_bytes=64)
+        key_words = keep.tile([P, B * N], U32, name="key_words", align_bytes=64)
+        key_scales = keep.tile([P, B * N], U8, name="key_scales", align_bytes=64)
+        warm_in = keep.tile([P, 1], F32, name="warm_in")
+        warm_out = keep.tile([P, 1], F32, name="warm_out")
+        q_raw = [keep.tile([P, PACK, NQ], F32, name=f"q_raw{b}") for b in range(B)]
+        q_bf = [keep.tile([P, NQ, PACK], BF16, name=f"q_bf{b}", align_bytes=64) for b in range(B)]
+        q_words = [keep.tile([P, NQ], U32, name=f"q_words{b}", align_bytes=64) for b in range(B)]
+        q_scales = [keep.tile([P, NQ], U8, name=f"q_scales{b}", align_bytes=64) for b in range(B)]
+        scores = [psum.tile([P, N], F32, name=f"scores{b}") for b in range(B)]
+        neg_max = [keep.tile([P, 1], F32, name=f"neg_max{b}") for b in range(B)]
+        row_sum = [keep.tile([P, 1], F32, name=f"row_sum{b}") for b in range(B)]
+        inv_sum = [keep.tile([P, 1], F32, name=f"inv_sum{b}") for b in range(B)]
+        expd = [keep.tile([P, N], F32, name=f"expd{b}") for b in range(B)]
+        weights = [keep.tile([P, N], F32, name=f"weights{b}") for b in range(B)]
+        maps = [keep.tile([P, T], F32, name=f"map{b}") for b in range(B)]
+
+        def listed(first, count):
+            return offsets[:, first // PER_COL : (first + count) // PER_COL]
+
+        nc.sync.dma_start(offsets[:], offs)
+        nc.vector.memset(pool_scales[:].bitcast(I32), 0)
+        nc.gpsimd.memset(warm_in[:], 0.0)
+        nc.scalar.activation(out=warm_out[:], in_=warm_in[:], func=ACT.Exp)
+        for r in range(4):
+            nc.sync.dma_start(pool_scales[r:P:32, :].bitcast(I32), k_scales[0, r:16:4, :].bitcast(I32))
+        nc.sync.dma_start(pool_words[:].bitcast(I32), k_words[0].rearrange("p t r -> p (t r)").bitcast(I32))
+        for b in range(B):
+            nc.sync.dma_start(q_raw[b][:], qT[b].rearrange("(p j) w -> p j w", j=PACK))
+        for b in range(B):
+            nc.vector.memset(maps[b][:], 0.0)
+
+        for b in range(B):
+            nc.vector.tensor_copy(key_scales[:, b * N : (b + 1) * N], pool_scales[:].indirect(listed(b * N, N)))
+
+        def front(b):
+            nc.scalar.copy(out=q_bf[b][:], in_=q_raw[b][:].rearrange("p j w -> p w j"))
+            nc.vector.quantize_mx(
+                out=q_words[b][:].bitcast(FP8X4),
+                scales=q_scales[b][:],
+                in_=q_bf[b][:].rearrange("p w j -> p (w j)"),
+            )
+            for h in range(2):
+                first = b * N + h * HALF
+                nc.vector.tensor_copy(key_words[:, first : first + HALF], pool_words[:].indirect(listed(first, HALF)))
+                nc.tensor.matmul_mx(
+                    out=scores[b][:, h * HALF : (h + 1) * HALF],
+                    lhsT=q_words[b][:].bitcast(FP8X4),
+                    lhsT_scale=q_scales[b][:],
+                    rhs=key_words[:, first : first + HALF].bitcast(FP8X4),
+                    rhs_scale=key_scales[:, first : first + HALF],
+                    start=True,
+                    stop=True,
+                )
+            nc.vector.tensor_reduce(out=neg_max[b][:], in_=scores[b][:], axis=AXIS.X, op=ALU.max, negate=True)
+            nc.scalar.activation(
+                out=expd[b][:], in_=scores[b][:], func=ACT.Exp, bias=neg_max[b][:], accum_out=row_sum[b][:]
+            )
+            nc.vector.reciprocal(inv_sum[b][:], row_sum[b][:])
+            nc.scalar.activation(out=weights[b][:], in_=expd[b][:], func=ACT.Copy, scale=inv_sum[b][:])
+
+        def scatter(b, h):
+            nc.vector.tensor_copy(
+                maps[b][:].indirect(listed(b * N + h * HALF, HALF)), weights[b][:, h * HALF : (h + 1) * HALF]
+            )
+
+        front(0)
+        scatter(0, 0)
+        front(1)
+        scatter(0, 1)
+        nc.sync.dma_start(out[0], maps[0][:])
+        scatter(1, 0)
+        scatter(1, 1)
+        nc.sync.dma_start(out[1], maps[1][:])

@@ -31,7 +31,7 @@ def tile_attend_wscat_topk_kernel(tc, qT, k_words, k_scales, offs, out):
         offsets = keep.tile([P, B * N // PER_COL], U16, name="offsets")
         pool_words = keep.tile([P, T], U32, name="pool_words", align_bytes=64)
         pool_scales = keep.tile([P, T], U8, name="pool_scales", align_bytes=64)
-        key_words = keep.tile([P, B * N], U32, name="key_words", align_bytes=64)
+        key_words = [keep.tile([P, HALF], U32, name=f"key_words{i}", align_bytes=64) for i in range(3)]
         key_scales = keep.tile([P, B * N], U8, name="key_scales", align_bytes=64)
         warm_in = keep.tile([P, 1], F32, name="warm_in")
         warm_out = keep.tile([P, 1], F32, name="warm_out")
@@ -40,67 +40,77 @@ def tile_attend_wscat_topk_kernel(tc, qT, k_words, k_scales, offs, out):
         q_words = [keep.tile([P, NQ], U32, name=f"q_words{b}", align_bytes=64) for b in range(B)]
         q_scales = [keep.tile([P, NQ], U8, name=f"q_scales{b}", align_bytes=64) for b in range(B)]
         scores = [psum.tile([P, N], F32, name=f"scores{b}") for b in range(B)]
-        neg_max = [keep.tile([P, 1], F32, name=f"neg_max{b}") for b in range(B)]
-        row_sum = [keep.tile([P, 1], F32, name=f"row_sum{b}") for b in range(B)]
-        inv_sum = [keep.tile([P, 1], F32, name=f"inv_sum{b}") for b in range(B)]
         expd = [keep.tile([P, N], F32, name=f"expd{b}") for b in range(B)]
         weights = [keep.tile([P, N], F32, name=f"weights{b}") for b in range(B)]
         maps = [keep.tile([P, T], F32, name=f"map{b}") for b in range(B)]
+        neg_max0 = keep.tile([P, 1], F32, name="neg_max0")
+        row_sum1 = keep.tile([P, 1], F32, name="row_sum1")
+        shared = weights[0][:, N - 1 : N]
+        neg_max = [neg_max0[:], shared]
+        row_sum = [shared, row_sum1[:]]
+        inv_sum = [keep.tile([P, 1], F32, name=f"inv_sum{b}") for b in range(B)]
+        key_slot = {(0, 0): 0, (0, 1): 1, (1, 0): 2, (1, 1): 1}
 
         def listed(first, count):
             return offsets[:, first // PER_COL : (first + count) // PER_COL]
 
+        def load_q(b):
+            nc.sync.dma_start(q_raw[b][:], qT[b].rearrange("(p j) w -> p j w", j=PACK))
+
         nc.sync.dma_start(offsets[:], offs)
+        load_q(0)
         nc.vector.memset(pool_scales[:].bitcast(I32), 0)
         nc.gpsimd.memset(warm_in[:], 0.0)
         nc.scalar.activation(out=warm_out[:], in_=warm_in[:], func=ACT.Exp)
         for r in range(4):
             nc.sync.dma_start(pool_scales[r:P:32, :].bitcast(I32), k_scales[0, r:16:4, :].bitcast(I32))
+        load_q(1)
         nc.sync.dma_start(pool_words[:].bitcast(I32), k_words[0].rearrange("p t r -> p (t r)").bitcast(I32))
         for b in range(B):
-            nc.sync.dma_start(q_raw[b][:], qT[b].rearrange("(p j) w -> p j w", j=PACK))
-        for b in range(B):
-            nc.vector.memset(maps[b][:], 0.0)
+            nc.vector.memset(maps[b][:].bitcast(I32), 0)
 
         for b in range(B):
             nc.vector.tensor_copy(key_scales[:, b * N : (b + 1) * N], pool_scales[:].indirect(listed(b * N, N)))
-
-        def front(b):
+        for b in range(B):
             nc.scalar.copy(out=q_bf[b][:], in_=q_raw[b][:].rearrange("p j w -> p w j"))
             nc.vector.quantize_mx(
                 out=q_words[b][:].bitcast(FP8X4),
                 scales=q_scales[b][:],
                 in_=q_bf[b][:].rearrange("p w j -> p (w j)"),
             )
-            for h in range(2):
-                first = b * N + h * HALF
-                nc.vector.tensor_copy(key_words[:, first : first + HALF], pool_words[:].indirect(listed(first, HALF)))
-                nc.tensor.matmul_mx(
-                    out=scores[b][:, h * HALF : (h + 1) * HALF],
-                    lhsT=q_words[b][:].bitcast(FP8X4),
-                    lhsT_scale=q_scales[b][:],
-                    rhs=key_words[:, first : first + HALF].bitcast(FP8X4),
-                    rhs_scale=key_scales[:, first : first + HALF],
-                    start=True,
-                    stop=True,
-                )
-            nc.vector.tensor_reduce(out=neg_max[b][:], in_=scores[b][:], axis=AXIS.X, op=ALU.max, negate=True)
-            nc.scalar.activation(
-                out=expd[b][:], in_=scores[b][:], func=ACT.Exp, bias=neg_max[b][:], accum_out=row_sum[b][:]
-            )
-            nc.vector.reciprocal(inv_sum[b][:], row_sum[b][:])
-            nc.scalar.activation(out=weights[b][:], in_=expd[b][:], func=ACT.Copy, scale=inv_sum[b][:])
 
-        def scatter(b, h):
-            nc.vector.tensor_copy(
-                maps[b][:].indirect(listed(b * N + h * HALF, HALF)), weights[b][:, h * HALF : (h + 1) * HALF]
+        def score(b, h):
+            first = b * N + h * HALF
+            words = key_words[key_slot[b, h]]
+            nc.vector.tensor_copy(words[:], pool_words[:].indirect(listed(first, HALF)))
+            nc.tensor.matmul_mx(
+                out=scores[b][:, h * HALF : (h + 1) * HALF],
+                lhsT=q_words[b][:].bitcast(FP8X4),
+                lhsT_scale=q_scales[b][:],
+                rhs=words[:].bitcast(FP8X4),
+                rhs_scale=key_scales[:, first : first + HALF],
+                start=True,
+                stop=True,
             )
 
-        front(0)
-        scatter(0, 0)
-        front(1)
-        scatter(0, 1)
+        def exponentiate(b):
+            nc.vector.tensor_reduce(out=neg_max[b], in_=scores[b][:], axis=AXIS.X, op=ALU.max, negate=True)
+            nc.scalar.activation(out=expd[b][:], in_=scores[b][:], func=ACT.Exp, bias=neg_max[b], accum_out=row_sum[b])
+            nc.vector.reciprocal(inv_sum[b][:], row_sum[b])
+
+        def place(b, first, count):
+            cols = slice(first, first + count)
+            nc.scalar.activation(out=weights[b][:, cols], in_=expd[b][:, cols], func=ACT.Copy, scale=inv_sum[b][:])
+            nc.vector.tensor_copy(maps[b][:].indirect(listed(b * N + first, count)), weights[b][:, cols])
+
+        score(0, 0)
+        score(0, 1)
+        score(1, 0)
+        exponentiate(0)
+        score(1, 1)
+        place(0, 0, HALF)
+        exponentiate(1)
+        place(0, HALF, HALF)
         nc.sync.dma_start(out[0], maps[0][:])
-        scatter(1, 0)
-        scatter(1, 1)
+        place(1, 0, N)
         nc.sync.dma_start(out[1], maps[1][:])

@@ -33,8 +33,6 @@ def tile_attend_wscat_topk_kernel(tc, qT, k_words, k_scales, offs, out):
         pool_scales = keep.tile([P, T], U8, name="pool_scales", align_bytes=64)
         key_words = [keep.tile([P, HALF], U32, name=f"key_words{i}", align_bytes=64) for i in range(3)]
         key_scales = keep.tile([P, B * N], U8, name="key_scales", align_bytes=64)
-        warm_in = keep.tile([P, 1], F32, name="warm_in")
-        warm_out = keep.tile([P, 1], F32, name="warm_out")
         q_raw = [keep.tile([P, PACK, NQ], F32, name=f"q_raw{b}") for b in range(B)]
         q_bf = [keep.tile([P, NQ, PACK], BF16, name=f"q_bf{b}", align_bytes=64) for b in range(B)]
         q_words = [keep.tile([P, NQ], U32, name=f"q_words{b}", align_bytes=64) for b in range(B)]
@@ -59,15 +57,14 @@ def tile_attend_wscat_topk_kernel(tc, qT, k_words, k_scales, offs, out):
 
         nc.sync.dma_start(offsets[:], offs)
         load_q(0)
-        nc.vector.memset(pool_scales[:].bitcast(I32), 0)
-        nc.gpsimd.memset(warm_in[:], 0.0)
-        nc.scalar.activation(out=warm_out[:], in_=warm_in[:], func=ACT.Exp)
+        nc.gpsimd.memset(pool_scales[:].bitcast(I32), 0)
         for r in range(4):
-            nc.sync.dma_start(pool_scales[r:P:32, :].bitcast(I32), k_scales[0, r:16:4, :].bitcast(I32))
+            queue = nc.sync if r % 2 == 0 else nc.scalar
+            queue.dma_start(pool_scales[r:P:32, :].bitcast(I32), k_scales[0, r:16:4, :].bitcast(I32))
         load_q(1)
         nc.sync.dma_start(pool_words[:].bitcast(I32), k_words[0].rearrange("p t r -> p (t r)").bitcast(I32))
         for b in range(B):
-            nc.vector.memset(maps[b][:].bitcast(I32), 0)
+            nc.gpsimd.memset(maps[b][:], 0.0)
 
         for b in range(B):
             nc.vector.tensor_copy(key_scales[:, b * N : (b + 1) * N], pool_scales[:].indirect(listed(b * N, N)))

@@ -20,6 +20,7 @@ P = 128
 PACK = 4
 HALF = N // 2
 PER_COL = 16
+PIECE = 512
 
 
 def tile_attend_wscat_topk_kernel(tc, qT, k_words, k_scales, offs, out):
@@ -31,7 +32,7 @@ def tile_attend_wscat_topk_kernel(tc, qT, k_words, k_scales, offs, out):
         offsets = keep.tile([P, B * N // PER_COL], U16, name="offsets")
         pool_words = keep.tile([P, T], U32, name="pool_words", align_bytes=64)
         pool_scales = keep.tile([P, T], U8, name="pool_scales", align_bytes=64)
-        key_words = [keep.tile([P, HALF], U32, name=f"key_words{i}", align_bytes=64) for i in range(3)]
+        key_words = [keep.tile([P, HALF], U32, name=f"key_words{i}", align_bytes=64) for i in range(2 * B)]
         key_scales = keep.tile([P, B * N], U8, name="key_scales", align_bytes=64)
         q_raw = [keep.tile([P, PACK, NQ], F32, name=f"q_raw{b}") for b in range(B)]
         q_bf = [keep.tile([P, NQ, PACK], BF16, name=f"q_bf{b}", align_bytes=64) for b in range(B)]
@@ -39,15 +40,13 @@ def tile_attend_wscat_topk_kernel(tc, qT, k_words, k_scales, offs, out):
         q_scales = [keep.tile([P, NQ], U8, name=f"q_scales{b}", align_bytes=64) for b in range(B)]
         scores = [psum.tile([P, N], F32, name=f"scores{b}") for b in range(B)]
         expd = [keep.tile([P, N], F32, name=f"expd{b}") for b in range(B)]
-        weights = [keep.tile([P, N], F32, name=f"weights{b}") for b in range(B)]
+        weights1 = keep.tile([P, N], F32, name="weights1")
         maps = [keep.tile([P, T], F32, name=f"map{b}") for b in range(B)]
-        neg_max0 = keep.tile([P, 1], F32, name="neg_max0")
-        row_sum1 = keep.tile([P, 1], F32, name="row_sum1")
-        shared = weights[0][:, N - 1 : N]
-        neg_max = [neg_max0[:], shared]
-        row_sum = [shared, row_sum1[:]]
+        divided = [keep.tile([P, PIECE], F32, name=f"divided{i}") for i in range(T // PIECE)]
+        neg_max = [keep.tile([P, 1], F32, name=f"neg_max{b}") for b in range(B)]
+        part_sum = weights1[:, N - 1 : N]
+        row_sum = [keep.tile([P, 1], F32, name=f"row_sum{b}") for b in range(B)]
         inv_sum = [keep.tile([P, 1], F32, name=f"inv_sum{b}") for b in range(B)]
-        key_slot = {(0, 0): 0, (0, 1): 1, (1, 0): 2, (1, 1): 1}
 
         def listed(first, count):
             return offsets[:, first // PER_COL : (first + count) // PER_COL]
@@ -76,38 +75,43 @@ def tile_attend_wscat_topk_kernel(tc, qT, k_words, k_scales, offs, out):
                 in_=q_bf[b][:].rearrange("p w j -> p (w j)"),
             )
 
-        def score(b, h):
-            first = b * N + h * HALF
-            words = key_words[key_slot[b, h]]
-            nc.vector.tensor_copy(words[:], pool_words[:].indirect(listed(first, HALF)))
-            nc.tensor.matmul_mx(
-                out=scores[b][:, h * HALF : (h + 1) * HALF],
-                lhsT=q_words[b][:].bitcast(FP8X4),
-                lhsT_scale=q_scales[b][:],
-                rhs=words[:].bitcast(FP8X4),
-                rhs_scale=key_scales[:, first : first + HALF],
-                start=True,
-                stop=True,
-            )
+        for b in range(B):
+            for h in range(2):
+                first = b * N + h * HALF
+                words = key_words[2 * b + h]
+                nc.vector.tensor_copy(words[:], pool_words[:].indirect(listed(first, HALF)))
+                nc.tensor.matmul_mx(
+                    out=scores[b][:, h * HALF : (h + 1) * HALF],
+                    lhsT=q_words[b][:].bitcast(FP8X4),
+                    lhsT_scale=q_scales[b][:],
+                    rhs=words[:].bitcast(FP8X4),
+                    rhs_scale=key_scales[:, first : first + HALF],
+                    start=True,
+                    stop=True,
+                )
 
-        def exponentiate(b):
-            nc.vector.tensor_reduce(out=neg_max[b], in_=scores[b][:], axis=AXIS.X, op=ALU.max, negate=True)
-            nc.scalar.activation(out=expd[b][:], in_=scores[b][:], func=ACT.Exp, bias=neg_max[b], accum_out=row_sum[b])
-            nc.vector.reciprocal(inv_sum[b][:], row_sum[b])
+        for b in range(B):
+            nc.vector.tensor_reduce(out=neg_max[b][:], in_=scores[b][:], axis=AXIS.X, op=ALU.max, negate=True)
 
-        def place(b, first, count):
-            cols = slice(first, first + count)
-            nc.scalar.activation(out=weights[b][:, cols], in_=expd[b][:, cols], func=ACT.Copy, scale=inv_sum[b][:])
-            nc.vector.tensor_copy(maps[b][:].indirect(listed(b * N + first, count)), weights[b][:, cols])
-
-        score(0, 0)
-        score(0, 1)
-        score(1, 0)
-        exponentiate(0)
-        score(1, 1)
-        place(0, 0, HALF)
-        exponentiate(1)
-        place(0, HALF, HALF)
-        nc.sync.dma_start(out[0], maps[0][:])
-        place(1, 0, N)
+        lower, upper = slice(0, HALF), slice(HALF, N)
+        nc.scalar.activation(
+            out=expd[0][:, lower], in_=scores[0][:, lower], func=ACT.Exp, bias=neg_max[0][:], accum_out=part_sum
+        )
+        nc.vector.tensor_copy(maps[0][:].indirect(listed(0, HALF)), expd[0][:, lower])
+        nc.scalar.activation(
+            out=expd[1][:], in_=scores[1][:], func=ACT.Exp, bias=neg_max[1][:], accum_out=row_sum[1][:]
+        )
+        nc.vector.reciprocal(inv_sum[1][:], row_sum[1][:])
+        nc.scalar.activation(
+            out=expd[0][:, upper], in_=scores[0][:, upper], func=ACT.Exp, bias=neg_max[0][:], accum_out=neg_max[1][:]
+        )
+        nc.scalar.activation(out=row_sum[0][:], in_=part_sum, func=ACT.Identity, bias=neg_max[1][:])
+        nc.vector.tensor_copy(maps[0][:].indirect(listed(HALF, HALF)), expd[0][:, upper])
+        nc.vector.reciprocal(inv_sum[0][:], row_sum[0][:])
+        nc.scalar.activation(out=weights1[:], in_=expd[1][:], func=ACT.Copy, scale=inv_sum[1][:])
+        nc.vector.tensor_copy(maps[1][:].indirect(listed(N, N)), weights1[:])
+        for i in range(T // PIECE):
+            cols = slice(i * PIECE, (i + 1) * PIECE)
+            nc.scalar.activation(out=divided[i][:], in_=maps[0][:, cols], func=ACT.Copy, scale=inv_sum[0][:])
+            nc.scalar.dma_start(out[0][:, cols], divided[i][:])
         nc.sync.dma_start(out[1], maps[1][:])

@@ -112,6 +112,9 @@ def tile_attend_wscat_topk_kernel(tc, qT, k_words, k_scales, offs, out):
         nc.vector.tensor_copy(maps[1][:].indirect(listed(N, N)), weights1[:])
         for i in range(T // PIECE):
             cols = slice(i * PIECE, (i + 1) * PIECE)
-            nc.scalar.activation(out=divided[i][:], in_=maps[0][:, cols], func=ACT.Copy, scale=inv_sum[0][:])
+            if i % 2 == 0:
+                nc.scalar.activation(out=divided[i][:], in_=maps[0][:, cols], func=ACT.Copy, scale=inv_sum[0][:])
+            else:
+                nc.gpsimd.tensor_scalar(divided[i][:], maps[0][:, cols], inv_sum[0][:], 0.0, ALU.mult, ALU.add)
             nc.scalar.dma_start(out[0][:, cols], divided[i][:])
         nc.sync.dma_start(out[1], maps[1][:])

@@ -27,14 +27,19 @@ def tile_attend_wscat_topk_kernel(tc, qT, k_words, k_scales, offs, out):
     nc = tc.nc
     with ExitStack() as ctx:
         keep = ctx.enter_context(tc.tile_pool(name="keep", bufs=1))
+        reused = ctx.enter_context(tc.tile_pool(name="reused", bufs=1))
         psum = ctx.enter_context(tc.psum_pool(name="psum", bufs=1))
 
         offsets = keep.tile([P, B * N // PER_COL], U16, name="offsets")
         pool_words = keep.tile([P, T], U32, name="pool_words", align_bytes=64)
         pool_scales = keep.tile([P, T], U8, name="pool_scales", align_bytes=64)
-        key_words = [keep.tile([P, HALF], U32, name=f"key_words{i}", align_bytes=64) for i in range(2 * B)]
+        key_words = [keep.tile([P, HALF], U32, name=f"key_words{i}", align_bytes=64) for i in range(2 * B - 1)]
         key_scales = keep.tile([P, B * N], U8, name="key_scales", align_bytes=64)
-        q_raw = [keep.tile([P, PACK, NQ], F32, name=f"q_raw{b}") for b in range(B)]
+        q_raw = [
+            keep.tile([P, PACK, NQ], F32, name="q_raw0"),
+            reused.tile([P, PACK, NQ], F32, name="q_raw1", offset=0, align_bytes=64),
+        ]
+        key_words.append(reused.tile([P, HALF], U32, name="key_words3", offset=0, align_bytes=64))
         q_bf = [keep.tile([P, NQ, PACK], BF16, name=f"q_bf{b}", align_bytes=64) for b in range(B)]
         q_words = [keep.tile([P, NQ], U32, name=f"q_words{b}", align_bytes=64) for b in range(B)]
         q_scales = [keep.tile([P, NQ], U8, name=f"q_scales{b}", align_bytes=64) for b in range(B)]
@@ -43,7 +48,10 @@ def tile_attend_wscat_topk_kernel(tc, qT, k_words, k_scales, offs, out):
         weights1 = keep.tile([P, N], F32, name="weights1")
         maps = [keep.tile([P, T], F32, name=f"map{b}") for b in range(B)]
         divided = [keep.tile([P, PIECE], F32, name=f"divided{i}") for i in range(T // PIECE)]
-        neg_max = [keep.tile([P, 1], F32, name=f"neg_max{b}") for b in range(B)]
+        neg_max = [
+            reused.tile([P, 1], F32, name="neg_max0", offset=4 * HALF, align_bytes=64),
+            keep.tile([P, 1], F32, name="neg_max1"),
+        ]
         part_sum = weights1[:, N - 1 : N]
         row_sum = [keep.tile([P, 1], F32, name=f"row_sum{b}") for b in range(B)]
         inv_sum = [keep.tile([P, 1], F32, name=f"inv_sum{b}") for b in range(B)]
@@ -60,8 +68,8 @@ def tile_attend_wscat_topk_kernel(tc, qT, k_words, k_scales, offs, out):
         for r in range(4):
             queue = nc.sync if r % 2 == 0 else nc.scalar
             queue.dma_start(pool_scales[r:P:32, :].bitcast(I32), k_scales[0, r:16:4, :].bitcast(I32))
-        load_q(1)
         nc.sync.dma_start(pool_words[:].bitcast(I32), k_words[0].rearrange("p t r -> p (t r)").bitcast(I32))
+        load_q(1)
         for b in range(B):
             nc.gpsimd.memset(maps[b][:], 0.0)
 

@@ -63,11 +63,13 @@ def tile_attend_wscat_topk_kernel(tc, qT, k_words, k_scales, offs, out):
             nc.sync.dma_start(q_raw[b][:], qT[b].rearrange("(p j) w -> p j w", j=PACK))
 
         nc.sync.dma_start(offsets[:], offs)
-        load_q(0)
+        q0_rows = qT[0].rearrange("(p j) w -> p j w", j=PACK)
+        nc.sync.dma_start(q_raw[0][:, :1, :], q0_rows[:, :1, :])
         nc.gpsimd.memset(pool_scales[:].bitcast(I32), 0)
         for r in range(4):
             queue = nc.sync if r % 2 == 0 else nc.scalar
             queue.dma_start(pool_scales[r:P:32, :].bitcast(I32), k_scales[0, r:16:4, :].bitcast(I32))
+        nc.sync.dma_start(q_raw[0][:, 1:, :], q0_rows[:, 1:, :])
         nc.sync.dma_start(pool_words[:].bitcast(I32), k_words[0].rearrange("p t r -> p (t r)").bitcast(I32))
         load_q(1)
         for b in range(B):

@@ -33,13 +33,16 @@ def tile_attend_wscat_topk_kernel(tc, qT, k_words, k_scales, offs, out):
         offsets = keep.tile([P, B * N // PER_COL], U16, name="offsets")
         pool_words = keep.tile([P, T], U32, name="pool_words", align_bytes=64)
         pool_scales = keep.tile([P, T], U8, name="pool_scales", align_bytes=64)
-        key_words = [keep.tile([P, HALF], U32, name=f"key_words{i}", align_bytes=64) for i in range(2 * B - 1)]
+        key_words = [
+            keep.tile([P, N], U32, name="key_words0", align_bytes=64),
+            keep.tile([P, HALF], U32, name="key_words1", align_bytes=64),
+        ]
         key_scales = keep.tile([P, B * N], U8, name="key_scales", align_bytes=64)
         q_raw = [
             keep.tile([P, PACK, NQ], F32, name="q_raw0"),
             reused.tile([P, PACK, NQ], F32, name="q_raw1", offset=0, align_bytes=64),
         ]
-        key_words.append(reused.tile([P, HALF], U32, name="key_words3", offset=0, align_bytes=64))
+        key_words.append(reused.tile([P, HALF], U32, name="key_words2", offset=0, align_bytes=64))
         q_bf = [keep.tile([P, NQ, PACK], BF16, name=f"q_bf{b}", align_bytes=64) for b in range(B)]
         q_words = [keep.tile([P, NQ], U32, name=f"q_words{b}", align_bytes=64) for b in range(B)]
         q_scales = [keep.tile([P, NQ], U8, name=f"q_scales{b}", align_bytes=64) for b in range(B)]
@@ -52,9 +55,11 @@ def tile_attend_wscat_topk_kernel(tc, qT, k_words, k_scales, offs, out):
             reused.tile([P, 1], F32, name="neg_max0", offset=4 * HALF, align_bytes=64),
             keep.tile([P, 1], F32, name="neg_max1"),
         ]
-        part_sum = weights1[:, N - 1 : N]
-        row_sum = [keep.tile([P, 1], F32, name=f"row_sum{b}") for b in range(B)]
-        inv_sum = [keep.tile([P, 1], F32, name=f"inv_sum{b}") for b in range(B)]
+        row_sum = keep.tile([P, B], F32, name="row_sum")
+        one = keep.tile([P, B], F32, name="one")
+        minus_one = keep.tile([P, B], F32, name="minus_one")
+        inv_both = keep.tile([P, B], F32, name="inv_both")
+        inv_sum = [inv_both[:, b : b + 1] for b in range(B)]
 
         def listed(first, count):
             return offsets[:, first // PER_COL : (first + count) // PER_COL]
@@ -72,11 +77,12 @@ def tile_attend_wscat_topk_kernel(tc, qT, k_words, k_scales, offs, out):
         nc.sync.dma_start(q_raw[0][:, 1:, :], q0_rows[:, 1:, :])
         nc.sync.dma_start(pool_words[:].bitcast(I32), k_words[0].rearrange("p t r -> p (t r)").bitcast(I32))
         load_q(1)
+        nc.gpsimd.memset(one[:], 1.0)
+        nc.scalar.activation(out=minus_one[:], in_=one[:], func=ACT.Copy, scale=-1.0)
         for b in range(B):
             nc.gpsimd.memset(maps[b][:], 0.0)
 
-        for b in range(B):
-            nc.vector.tensor_copy(key_scales[:, b * N : (b + 1) * N], pool_scales[:].indirect(listed(b * N, N)))
+        nc.vector.tensor_copy(key_scales[:], pool_scales[:].indirect(offsets[:]))
         for b in range(B):
             nc.scalar.copy(out=q_bf[b][:], in_=q_raw[b][:].rearrange("p j w -> p w j"))
             nc.vector.quantize_mx(
@@ -85,46 +91,34 @@ def tile_attend_wscat_topk_kernel(tc, qT, k_words, k_scales, offs, out):
                 in_=q_bf[b][:].rearrange("p w j -> p (w j)"),
             )
 
-        for b in range(B):
-            for h in range(2):
-                first = b * N + h * HALF
-                words = key_words[2 * b + h]
-                nc.vector.tensor_copy(words[:], pool_words[:].indirect(listed(first, HALF)))
-                nc.tensor.matmul_mx(
-                    out=scores[b][:, h * HALF : (h + 1) * HALF],
-                    lhsT=q_words[b][:].bitcast(FP8X4),
-                    lhsT_scale=q_scales[b][:],
-                    rhs=words[:].bitcast(FP8X4),
-                    rhs_scale=key_scales[:, first : first + HALF],
-                    start=True,
-                    stop=True,
-                )
+        for words, (b, first, count) in zip(key_words, [(0, 0, N), (1, 0, HALF), (1, HALF, HALF)]):
+            nc.vector.tensor_copy(words[:], pool_words[:].indirect(listed(b * N + first, count)))
+            nc.tensor.matmul_mx(
+                out=scores[b][:, first : first + count],
+                lhsT=q_words[b][:].bitcast(FP8X4),
+                lhsT_scale=q_scales[b][:],
+                rhs=words[:].bitcast(FP8X4),
+                rhs_scale=key_scales[:, b * N + first : b * N + first + count],
+                start=True,
+                stop=True,
+            )
 
         for b in range(B):
             nc.vector.tensor_reduce(out=neg_max[b][:], in_=scores[b][:], axis=AXIS.X, op=ALU.max, negate=True)
 
-        lower, upper = slice(0, HALF), slice(HALF, N)
-        nc.scalar.activation(
-            out=expd[0][:, lower], in_=scores[0][:, lower], func=ACT.Exp, bias=neg_max[0][:], accum_out=part_sum
-        )
-        nc.vector.tensor_copy(maps[0][:].indirect(listed(0, HALF)), expd[0][:, lower])
-        nc.scalar.activation(
-            out=expd[1][:], in_=scores[1][:], func=ACT.Exp, bias=neg_max[1][:], accum_out=row_sum[1][:]
-        )
-        nc.vector.reciprocal(inv_sum[1][:], row_sum[1][:])
-        nc.scalar.activation(
-            out=expd[0][:, upper], in_=scores[0][:, upper], func=ACT.Exp, bias=neg_max[0][:], accum_out=neg_max[1][:]
-        )
-        nc.scalar.activation(out=row_sum[0][:], in_=part_sum, func=ACT.Identity, bias=neg_max[1][:])
-        nc.vector.tensor_copy(maps[0][:].indirect(listed(HALF, HALF)), expd[0][:, upper])
-        nc.vector.reciprocal(inv_sum[0][:], row_sum[0][:])
-        nc.scalar.activation(out=weights1[:], in_=expd[1][:], func=ACT.Copy, scale=inv_sum[1][:])
+        for b in range(B):
+            nc.scalar.activation(
+                out=expd[b][:], in_=scores[b][:], func=ACT.Exp, bias=neg_max[b][:], accum_out=row_sum[:, b : b + 1]
+            )
+        nc.gpsimd.tensor_tensor(inv_both[:], row_sum[:], minus_one[:], ALU.pow)
+        nc.vector.tensor_copy(maps[0][:].indirect(listed(0, N)), expd[0][:])
+        nc.scalar.activation(out=weights1[:], in_=expd[1][:], func=ACT.Copy, scale=inv_sum[1])
         nc.vector.tensor_copy(maps[1][:].indirect(listed(N, N)), weights1[:])
         for i in range(T // PIECE):
             cols = slice(i * PIECE, (i + 1) * PIECE)
             if i % 2 == 0:
-                nc.scalar.activation(out=divided[i][:], in_=maps[0][:, cols], func=ACT.Copy, scale=inv_sum[0][:])
+                nc.scalar.activation(out=divided[i][:], in_=maps[0][:, cols], func=ACT.Copy, scale=inv_sum[0])
             else:
-                nc.gpsimd.tensor_scalar(divided[i][:], maps[0][:, cols], inv_sum[0][:], 0.0, ALU.mult, ALU.add)
+                nc.gpsimd.tensor_scalar(divided[i][:], maps[0][:, cols], inv_sum[0], 0.0, ALU.mult, ALU.add)
             nc.scalar.dma_start(out[0][:, cols], divided[i][:])
         nc.sync.dma_start(out[1], maps[1][:])

@@ -43,13 +43,13 @@ def tile_attend_wscat_topk_kernel(tc, qT, k_words, k_scales, offs, out):
             reused.tile([P, PACK, NQ], F32, name="q_raw1", offset=0, align_bytes=64),
         ]
         key_words.append(reused.tile([P, HALF], U32, name="key_words2", offset=0, align_bytes=64))
-        q_bf = [keep.tile([P, NQ, PACK], BF16, name=f"q_bf{b}", align_bytes=64) for b in range(B)]
+        q_bf = [keep.tile([P, NQ, PACK], BF16, name=f"q_bf{b}", tag=f"q_bf{b}", align_bytes=64) for b in range(B)]
         q_words = [keep.tile([P, NQ], U32, name=f"q_words{b}", align_bytes=64) for b in range(B)]
         q_scales = [keep.tile([P, NQ], U8, name=f"q_scales{b}", align_bytes=64) for b in range(B)]
         scores = [psum.tile([P, N], F32, name=f"scores{b}") for b in range(B)]
         expd = [keep.tile([P, N], F32, name=f"expd{b}") for b in range(B)]
         weights1 = keep.tile([P, N], F32, name="weights1")
-        maps = [keep.tile([P, T], F32, name=f"map{b}") for b in range(B)]
+        maps = [keep.tile([P, T], F32, name="map0")]
         divided = [keep.tile([P, PIECE], F32, name=f"divided{i}") for i in range(T // PIECE)]
         neg_max = [
             reused.tile([P, 1], F32, name="neg_max0", offset=4 * HALF, align_bytes=64),
@@ -69,18 +69,17 @@ def tile_attend_wscat_topk_kernel(tc, qT, k_words, k_scales, offs, out):
 
         nc.sync.dma_start(offsets[:], offs)
         q0_rows = qT[0].rearrange("(p j) w -> p j w", j=PACK)
-        nc.sync.dma_start(q_raw[0][:, :1, :], q0_rows[:, :1, :])
-        nc.gpsimd.memset(pool_scales[:].bitcast(I32), 0)
+        nc.sync.dma_start(q_raw[0][:, :2, :], q0_rows[:, :2, :])
+        nc.vector.memset(pool_scales[:].bitcast(I32), 0)
         for r in range(4):
             queue = nc.sync if r % 2 == 0 else nc.scalar
             queue.dma_start(pool_scales[r:P:32, :].bitcast(I32), k_scales[0, r:16:4, :].bitcast(I32))
-        nc.sync.dma_start(q_raw[0][:, 1:, :], q0_rows[:, 1:, :])
+        nc.sync.dma_start(q_raw[0][:, 2:, :], q0_rows[:, 2:, :])
         nc.sync.dma_start(pool_words[:].bitcast(I32), k_words[0].rearrange("p t r -> p (t r)").bitcast(I32))
         load_q(1)
-        nc.gpsimd.memset(one[:], 1.0)
+        nc.vector.memset(one[:], 1.0)
         nc.scalar.activation(out=minus_one[:], in_=one[:], func=ACT.Copy, scale=-1.0)
-        for b in range(B):
-            nc.gpsimd.memset(maps[b][:], 0.0)
+        nc.vector.memset(maps[0][:], 0.0)
 
         nc.vector.tensor_copy(key_scales[:], pool_scales[:].indirect(offsets[:]))
         for b in range(B):
@@ -90,6 +89,9 @@ def tile_attend_wscat_topk_kernel(tc, qT, k_words, k_scales, offs, out):
                 scales=q_scales[b][:],
                 in_=q_bf[b][:].rearrange("p w j -> p (w j)"),
             )
+
+        maps.append(keep.tile([P, T], F32, name="map1", tag="q_bf1", align_bytes=64))
+        nc.gpsimd.memset(maps[1][:], 0.0)
 
         for words, (b, first, count) in zip(key_words, [(0, 0, N), (1, 0, HALF), (1, HALF, HALF)]):
             nc.vector.tensor_copy(words[:], pool_words[:].indirect(listed(b * N + first, count)))

@@ -123,4 +123,6 @@ def tile_attend_wscat_topk_kernel(tc, qT, k_words, k_scales, offs, out):
             else:
                 nc.gpsimd.tensor_scalar(divided[i][:], maps[0][:, cols], inv_sum[0], 0.0, ALU.mult, ALU.add)
             nc.scalar.dma_start(out[0][:, cols], divided[i][:])
-        nc.sync.dma_start(out[1], maps[1][:])
+        for half in range(2):
+            cols = slice(half * T // 2, (half + 1) * T // 2)
+            nc.sync.dma_start(out[1][:, cols], maps[1][:, cols])

@@ -67,14 +67,14 @@ def tile_attend_wscat_topk_kernel(tc, qT, k_words, k_scales, offs, out):
         def load_q(b):
             nc.sync.dma_start(q_raw[b][:], qT[b].rearrange("(p j) w -> p j w", j=PACK))
 
-        nc.sync.dma_start(offsets[:], offs)
         q0_rows = qT[0].rearrange("(p j) w -> p j w", j=PACK)
-        nc.sync.dma_start(q_raw[0][:, :2, :], q0_rows[:, :2, :])
+        nc.sync.dma_start(q_raw[0][:, :3, :], q0_rows[:, :3, :])
+        nc.sync.dma_start(offsets[:], offs)
         nc.vector.memset(pool_scales[:].bitcast(I32), 0)
         for r in range(4):
             queue = nc.sync if r % 2 == 0 else nc.scalar
             queue.dma_start(pool_scales[r:P:32, :].bitcast(I32), k_scales[0, r:16:4, :].bitcast(I32))
-        nc.sync.dma_start(q_raw[0][:, 2:, :], q0_rows[:, 2:, :])
+        nc.sync.dma_start(q_raw[0][:, 3:, :], q0_rows[:, 3:, :])
         nc.sync.dma_start(pool_words[:].bitcast(I32), k_words[0].rearrange("p t r -> p (t r)").bitcast(I32))
         load_q(1)
         nc.vector.memset(one[:], 1.0)

@@ -72,8 +72,7 @@ def tile_attend_wscat_topk_kernel(tc, qT, k_words, k_scales, offs, out):
         nc.sync.dma_start(offsets[:], offs)
         nc.vector.memset(pool_scales[:].bitcast(I32), 0)
         for r in range(4):
-            queue = nc.sync if r % 2 == 0 else nc.scalar
-            queue.dma_start(pool_scales[r:P:32, :].bitcast(I32), k_scales[0, r:16:4, :].bitcast(I32))
+            nc.sync.dma_start(pool_scales[r:P:32, :].bitcast(I32), k_scales[0, r:16:4, :].bitcast(I32))
         nc.sync.dma_start(q_raw[0][:, 3:, :], q0_rows[:, 3:, :])
         nc.sync.dma_start(pool_words[:].bitcast(I32), k_words[0].rearrange("p t r -> p (t r)").bitcast(I32))
         load_q(1)

@@ -21,6 +21,9 @@ PACK = 4
 HALF = N // 2
 PER_COL = 16
 PIECE = 512
+ROWS = D // 32
+LIVE = P - ROWS
+EARLY = N + HALF
 
 
 def tile_attend_wscat_topk_kernel(tc, qT, k_words, k_scales, offs, out):
@@ -33,16 +36,14 @@ def tile_attend_wscat_topk_kernel(tc, qT, k_words, k_scales, offs, out):
         offsets = keep.tile([P, B * N // PER_COL], U16, name="offsets")
         pool_words = keep.tile([P, T], U32, name="pool_words", align_bytes=64)
         pool_scales = keep.tile([P, T], U8, name="pool_scales", align_bytes=64)
-        key_words = [
-            keep.tile([P, N], U32, name="key_words0", align_bytes=64),
-            keep.tile([P, HALF], U32, name="key_words1", align_bytes=64),
-        ]
+        early_words = keep.tile([P, EARLY], U32, name="early_words", align_bytes=64)
+        key_rows = keep.tile([P, B * N], U8, name="key_rows", align_bytes=64)
         key_scales = keep.tile([P, B * N], U8, name="key_scales", align_bytes=64)
+        raw_bytes = 4 * PACK * NQ
         q_raw = [
-            keep.tile([P, PACK, NQ], F32, name="q_raw0"),
-            reused.tile([P, PACK, NQ], F32, name="q_raw1", offset=0, align_bytes=64),
+            reused.tile([P, PACK, NQ], F32, name=f"q_raw{b}", offset=b * raw_bytes, align_bytes=64) for b in range(B)
         ]
-        key_words.append(reused.tile([P, HALF], U32, name="key_words2", offset=0, align_bytes=64))
+        late_words = reused.tile([P, HALF], U32, name="late_words", offset=0, align_bytes=64)
         q_bf = [keep.tile([P, NQ, PACK], BF16, name=f"q_bf{b}", tag=f"q_bf{b}", align_bytes=64) for b in range(B)]
         q_words = [keep.tile([P, NQ], U32, name=f"q_words{b}", align_bytes=64) for b in range(B)]
         q_scales = [keep.tile([P, NQ], U8, name=f"q_scales{b}", align_bytes=64) for b in range(B)]
@@ -52,7 +53,7 @@ def tile_attend_wscat_topk_kernel(tc, qT, k_words, k_scales, offs, out):
         maps = [keep.tile([P, T], F32, name="map0")]
         divided = [keep.tile([P, PIECE], F32, name=f"divided{i}") for i in range(T // PIECE)]
         neg_max = [
-            reused.tile([P, 1], F32, name="neg_max0", offset=4 * HALF, align_bytes=64),
+            reused.tile([P, 1], F32, name="neg_max0", offset=raw_bytes, align_bytes=64),
             keep.tile([P, 1], F32, name="neg_max1"),
         ]
         row_sum = keep.tile([P, B], F32, name="row_sum")
@@ -64,24 +65,24 @@ def tile_attend_wscat_topk_kernel(tc, qT, k_words, k_scales, offs, out):
         def listed(first, count):
             return offsets[:, first // PER_COL : (first + count) // PER_COL]
 
-        def load_q(b):
-            nc.sync.dma_start(q_raw[b][:], qT[b].rearrange("(p j) w -> p j w", j=PACK))
-
-        q0_rows = qT[0].rearrange("(p j) w -> p j w", j=PACK)
-        nc.sync.dma_start(q_raw[0][:, :3, :], q0_rows[:, :3, :])
+        nc.sync.dma_start(pool_scales[LIVE:, :].bitcast(I32), k_scales[0].bitcast(I32))
         nc.sync.dma_start(offsets[:], offs)
-        nc.vector.memset(pool_scales[:].bitcast(I32), 0)
-        for r in range(4):
-            nc.sync.dma_start(pool_scales[r:P:32, :].bitcast(I32), k_scales[0, r:16:4, :].bitcast(I32))
-        nc.sync.dma_start(q_raw[0][:, 3:, :], q0_rows[:, 3:, :])
         nc.sync.dma_start(pool_words[:].bitcast(I32), k_words[0].rearrange("p t r -> p (t r)").bitcast(I32))
-        load_q(1)
+        for b in range(B):
+            nc.sync.dma_start(q_raw[b][:], qT[b].rearrange("(p j) w -> p j w", j=PACK))
+        nc.vector.memset(pool_scales[:LIVE, :].bitcast(I32), 0)
         nc.vector.memset(one[:], 1.0)
         nc.scalar.activation(out=minus_one[:], in_=one[:], func=ACT.Copy, scale=-1.0)
         nc.vector.memset(maps[0][:], 0.0)
 
-        nc.vector.tensor_copy(key_scales[:], pool_scales[:].indirect(offsets[:]))
-        for b in range(B):
+        nc.vector.tensor_copy(key_rows[:], pool_scales[:].indirect(offsets[:]))
+        for quad in range(4):
+            nc.sync.dma_start(
+                key_scales[32 * quad : 32 * quad + 4, :].bitcast(I32),
+                key_rows[LIVE + 4 * quad : LIVE + 4 * quad + 4, :].bitcast(I32),
+            )
+
+        def quantize(b):
             nc.scalar.copy(out=q_bf[b][:], in_=q_raw[b][:].rearrange("p j w -> p w j"))
             nc.vector.quantize_mx(
                 out=q_words[b][:].bitcast(FP8X4),
@@ -89,20 +90,28 @@ def tile_attend_wscat_topk_kernel(tc, qT, k_words, k_scales, offs, out):
                 in_=q_bf[b][:].rearrange("p w j -> p (w j)"),
             )
 
-        maps.append(keep.tile([P, T], F32, name="map1", tag="q_bf1", align_bytes=64))
-        nc.gpsimd.memset(maps[1][:], 0.0)
-
-        for words, (b, first, count) in zip(key_words, [(0, 0, N), (1, 0, HALF), (1, HALF, HALF)]):
-            nc.vector.tensor_copy(words[:], pool_words[:].indirect(listed(b * N + first, count)))
+        def score(b, first, words):
+            count = words.shape[1]
             nc.tensor.matmul_mx(
                 out=scores[b][:, first : first + count],
                 lhsT=q_words[b][:].bitcast(FP8X4),
                 lhsT_scale=q_scales[b][:],
-                rhs=words[:].bitcast(FP8X4),
+                rhs=words.bitcast(FP8X4),
                 rhs_scale=key_scales[:, b * N + first : b * N + first + count],
                 start=True,
                 stop=True,
             )
+
+        nc.vector.tensor_copy(early_words[:], pool_words[:].indirect(listed(0, EARLY)))
+        quantize(0)
+        score(0, 0, early_words[:, :N])
+        nc.vector.tensor_copy(late_words[:], pool_words[:].indirect(listed(EARLY, HALF)))
+        quantize(1)
+        score(1, 0, early_words[:, N:])
+        score(1, HALF, late_words[:])
+
+        maps.append(keep.tile([P, T], F32, name="map1", tag="q_bf1", align_bytes=64))
+        nc.gpsimd.memset(maps[1][:], 0.0)
 
         for b in range(B):
             nc.vector.tensor_reduce(out=neg_max[b][:], in_=scores[b][:], axis=AXIS.X, op=ALU.max, negate=True)

@@ -23,7 +23,6 @@ PER_COL = 16
 PIECE = 512
 ROWS = D // 32
 LIVE = P - ROWS
-EARLY = N + HALF
 
 
 def tile_attend_wscat_topk_kernel(tc, qT, k_words, k_scales, offs, out):
@@ -36,14 +35,16 @@ def tile_attend_wscat_topk_kernel(tc, qT, k_words, k_scales, offs, out):
         offsets = keep.tile([P, B * N // PER_COL], U16, name="offsets")
         pool_words = keep.tile([P, T], U32, name="pool_words", align_bytes=64)
         pool_scales = keep.tile([P, T], U8, name="pool_scales", align_bytes=64)
-        early_words = keep.tile([P, EARLY], U32, name="early_words", align_bytes=64)
+        early_words = keep.tile([P, N], U32, name="early_words", align_bytes=64)
         key_rows = keep.tile([P, B * N], U8, name="key_rows", align_bytes=64)
         key_scales = keep.tile([P, B * N], U8, name="key_scales", align_bytes=64)
         raw_bytes = 4 * PACK * NQ
         q_raw = [
             reused.tile([P, PACK, NQ], F32, name=f"q_raw{b}", offset=b * raw_bytes, align_bytes=64) for b in range(B)
         ]
-        late_words = reused.tile([P, HALF], U32, name="late_words", offset=0, align_bytes=64)
+        late_words = [
+            reused.tile([P, HALF], U32, name=f"late_words{h}", offset=h * raw_bytes, align_bytes=64) for h in range(2)
+        ]
         q_bf = [keep.tile([P, NQ, PACK], BF16, name=f"q_bf{b}", tag=f"q_bf{b}", align_bytes=64) for b in range(B)]
         q_words = [keep.tile([P, NQ], U32, name=f"q_words{b}", align_bytes=64) for b in range(B)]
         q_scales = [keep.tile([P, NQ], U8, name=f"q_scales{b}", align_bytes=64) for b in range(B)]
@@ -53,7 +54,7 @@ def tile_attend_wscat_topk_kernel(tc, qT, k_words, k_scales, offs, out):
         maps = [keep.tile([P, T], F32, name="map0")]
         divided = [keep.tile([P, PIECE], F32, name=f"divided{i}") for i in range(T // PIECE)]
         neg_max = [
-            reused.tile([P, 1], F32, name="neg_max0", offset=raw_bytes, align_bytes=64),
+            reused.tile([P, 1], F32, name="neg_max0", offset=raw_bytes + 4 * HALF, align_bytes=64),
             keep.tile([P, 1], F32, name="neg_max1"),
         ]
         row_sum = keep.tile([P, B], F32, name="row_sum")
@@ -102,13 +103,14 @@ def tile_attend_wscat_topk_kernel(tc, qT, k_words, k_scales, offs, out):
                 stop=True,
             )
 
-        nc.vector.tensor_copy(early_words[:], pool_words[:].indirect(listed(0, EARLY)))
+        nc.vector.tensor_copy(early_words[:], pool_words[:].indirect(listed(0, N)))
         quantize(0)
-        score(0, 0, early_words[:, :N])
-        nc.vector.tensor_copy(late_words[:], pool_words[:].indirect(listed(EARLY, HALF)))
+        score(0, 0, early_words[:])
+        nc.vector.tensor_copy(late_words[0][:], pool_words[:].indirect(listed(N, HALF)))
         quantize(1)
-        score(1, 0, early_words[:, N:])
-        score(1, HALF, late_words[:])
+        score(1, 0, late_words[0][:])
+        nc.vector.tensor_copy(late_words[1][:], pool_words[:].indirect(listed(N + HALF, HALF)))
+        score(1, HALF, late_words[1][:])
 
         maps.append(keep.tile([P, T], F32, name="map1", tag="q_bf1", align_bytes=64))
         nc.gpsimd.memset(maps[1][:], 0.0)

@@ -21,6 +21,7 @@ PACK = 4
 HALF = N // 2
 PER_COL = 16
 PIECE = 512
+LINE = 4
 ROWS = D // 32
 LIVE = P - ROWS
 
@@ -83,8 +84,18 @@ def tile_attend_wscat_topk_kernel(tc, qT, k_words, k_scales, offs, out):
                 key_rows[LIVE + 4 * quad : LIVE + 4 * quad + 4, :].bitcast(I32),
             )
 
+        def walk(b, cols):
+            return (
+                q_bf[b][:, cols, :].rearrange("p (c i) j -> p c j i", i=LINE),
+                q_raw[b][:, :, cols].rearrange("p j (c i) -> p c j i", i=LINE),
+            )
+
         def quantize(b):
-            nc.scalar.copy(out=q_bf[b][:], in_=q_raw[b][:].rearrange("p j w -> p w j"))
+            if b == 0:
+                nc.scalar.copy(*walk(b, slice(0, NQ // 2)))
+                nc.gpsimd.tensor_scalar(*walk(b, slice(NQ // 2, NQ)), 1.0, 0.0, ALU.mult, ALU.add)
+            else:
+                nc.scalar.copy(*walk(b, slice(0, NQ)))
             nc.vector.quantize_mx(
                 out=q_words[b][:].bitcast(FP8X4),
                 scales=q_scales[b][:],

@@ -91,11 +91,7 @@ def tile_attend_wscat_topk_kernel(tc, qT, k_words, k_scales, offs, out):
             )
 
         def quantize(b):
-            if b == 0:
-                nc.scalar.copy(*walk(b, slice(0, NQ // 2)))
-                nc.gpsimd.tensor_scalar(*walk(b, slice(NQ // 2, NQ)), 1.0, 0.0, ALU.mult, ALU.add)
-            else:
-                nc.scalar.copy(*walk(b, slice(0, NQ)))
+            nc.scalar.copy(*walk(b, slice(0, NQ)))
             nc.vector.quantize_mx(
                 out=q_words[b][:].bitcast(FP8X4),
                 scales=q_scales[b][:],

@@ -142,4 +142,4 @@ def tile_attend_wscat_topk_kernel(tc, qT, k_words, k_scales, offs, out):
             nc.scalar.dma_start(out[0][:, cols], divided[i][:])
         for half in range(2):
             cols = slice(half * T // 2, (half + 1) * T // 2)
-            nc.sync.dma_start(out[1][:, cols], maps[1][:, cols])
+            (nc.sync, nc.scalar)[half].dma_start(out[1][:, cols], maps[1][:, cols])

@@ -22,6 +22,7 @@ HALF = N // 2
 PER_COL = 16
 PIECE = 512
 LINE = 4
+GPSIMD_COLS = 24
 ROWS = D // 32
 LIVE = P - ROWS
 
@@ -39,23 +40,27 @@ def tile_attend_wscat_topk_kernel(tc, qT, k_words, k_scales, offs, out):
         early_words = keep.tile([P, N], U32, name="early_words", align_bytes=64)
         key_rows = keep.tile([P, B * N], U8, name="key_rows", align_bytes=64)
         key_scales = keep.tile([P, B * N], U8, name="key_scales", align_bytes=64)
-        raw_bytes = 4 * PACK * NQ
         q_raw = [
-            reused.tile([P, PACK, NQ], F32, name=f"q_raw{b}", offset=b * raw_bytes, align_bytes=64) for b in range(B)
+            reused.tile([P, PACK, NQ], F32, name="q_raw0", offset=64, align_bytes=64),
+            keep.tile([P, PACK, NQ], F32, name="q_raw1", align_bytes=64),
         ]
         late_words = [
-            reused.tile([P, HALF], U32, name=f"late_words{h}", offset=h * raw_bytes, align_bytes=64) for h in range(2)
+            reused.tile([P, HALF], U32, name=f"late_words{h}", offset=NQ + h * 4 * HALF, align_bytes=64)
+            for h in range(2)
         ]
         q_bf = [keep.tile([P, NQ, PACK], BF16, name=f"q_bf{b}", tag=f"q_bf{b}", align_bytes=64) for b in range(B)]
         q_words = [keep.tile([P, NQ], U32, name=f"q_words{b}", align_bytes=64) for b in range(B)]
-        q_scales = [keep.tile([P, NQ], U8, name=f"q_scales{b}", align_bytes=64) for b in range(B)]
+        q_scales = [
+            keep.tile([P, NQ], U8, name="q_scales0", align_bytes=64),
+            reused.tile([P, NQ], U8, name="q_scales1", offset=0, align_bytes=64),
+        ]
         scores = [psum.tile([P, N], F32, name=f"scores{b}") for b in range(B)]
         expd = [keep.tile([P, N], F32, name=f"expd{b}") for b in range(B)]
         weights1 = keep.tile([P, N], F32, name="weights1")
         maps = [keep.tile([P, T], F32, name="map0")]
         divided = [keep.tile([P, PIECE], F32, name=f"divided{i}") for i in range(T // PIECE)]
         neg_max = [
-            reused.tile([P, 1], F32, name="neg_max0", offset=raw_bytes + 4 * HALF, align_bytes=64),
+            keep.tile([P, 1], F32, name="neg_max0"),
             keep.tile([P, 1], F32, name="neg_max1"),
         ]
         row_sum = keep.tile([P, B], F32, name="row_sum")
@@ -91,7 +96,17 @@ def tile_attend_wscat_topk_kernel(tc, qT, k_words, k_scales, offs, out):
             )
 
         def quantize(b):
-            nc.scalar.copy(*walk(b, slice(0, NQ)))
+            shared = GPSIMD_COLS if b == 0 else 0
+            nc.scalar.copy(*walk(b, slice(0, NQ - shared)))
+            if shared:
+                nc.gpsimd.tensor_scalar(
+                    q_bf[b][:, NQ - shared :, :],
+                    q_raw[b][:, :, NQ - shared :].rearrange("p j w -> p w j"),
+                    1.0,
+                    0.0,
+                    ALU.mult,
+                    ALU.add,
+                )
             nc.vector.quantize_mx(
                 out=q_words[b][:].bitcast(FP8X4),
                 scales=q_scales[b][:],

@@ -35,7 +35,7 @@ def tile_attend_wscat_topk_kernel(tc, qT, k_words, k_scales, offs, out):
         psum = ctx.enter_context(tc.psum_pool(name="psum", bufs=1))
 
         offsets = keep.tile([P, B * N // PER_COL], U16, name="offsets")
-        pool_words = keep.tile([P, T], U32, name="pool_words", align_bytes=64)
+        pool_words = keep.tile([P, T], U32, name="pool_words", tag="pool_words", align_bytes=64)
         pool_scales = keep.tile([P, T], U8, name="pool_scales", align_bytes=64)
         early_words = keep.tile([P, N], U32, name="early_words", align_bytes=64)
         key_rows = keep.tile([P, B * N], U8, name="key_rows", align_bytes=64)
@@ -134,7 +134,7 @@ def tile_attend_wscat_topk_kernel(tc, qT, k_words, k_scales, offs, out):
         nc.vector.tensor_copy(late_words[1][:], pool_words[:].indirect(listed(N + HALF, HALF)))
         score(1, HALF, late_words[1][:])
 
-        maps.append(keep.tile([P, T], F32, name="map1", tag="q_bf1", align_bytes=64))
+        maps.append(keep.tile([P, T], F32, name="map1", tag="pool_words", align_bytes=64))
         nc.gpsimd.memset(maps[1][:], 0.0)
 
         for b in range(B):

@@ -20,7 +20,6 @@ P = 128
 PACK = 4
 HALF = N // 2
 PER_COL = 16
-PIECE = 512
 LINE = 4
 GPSIMD_COLS = 24
 ROWS = D // 32
@@ -58,7 +57,8 @@ def tile_attend_wscat_topk_kernel(tc, qT, k_words, k_scales, offs, out):
         expd = [keep.tile([P, N], F32, name=f"expd{b}") for b in range(B)]
         weights1 = keep.tile([P, N], F32, name="weights1")
         maps = [keep.tile([P, T], F32, name="map0")]
-        divided = [keep.tile([P, PIECE], F32, name=f"divided{i}") for i in range(T // PIECE)]
+        edges = (0, 384, 768, 1408, T)
+        divided = [keep.tile([P, edges[i + 1] - edges[i]], F32, name=f"divided{i}") for i in range(len(edges) - 1)]
         neg_max = [
             keep.tile([P, 1], F32, name="neg_max0"),
             keep.tile([P, 1], F32, name="neg_max1"),
@@ -148,13 +148,13 @@ def tile_attend_wscat_topk_kernel(tc, qT, k_words, k_scales, offs, out):
         nc.vector.tensor_copy(maps[0][:].indirect(listed(0, N)), expd[0][:])
         nc.scalar.activation(out=weights1[:], in_=expd[1][:], func=ACT.Copy, scale=inv_sum[1])
         nc.vector.tensor_copy(maps[1][:].indirect(listed(N, N)), weights1[:])
-        for i in range(T // PIECE):
-            cols = slice(i * PIECE, (i + 1) * PIECE)
+        for i in range(len(divided)):
+            cols = slice(edges[i], edges[i + 1])
             if i % 2 == 0:
                 nc.scalar.activation(out=divided[i][:], in_=maps[0][:, cols], func=ACT.Copy, scale=inv_sum[0])
             else:
                 nc.gpsimd.tensor_scalar(divided[i][:], maps[0][:, cols], inv_sum[0], 0.0, ALU.mult, ALU.add)
-            nc.scalar.dma_start(out[0][:, cols], divided[i][:])
+            (nc.sync if i == 1 else nc.scalar).dma_start(out[0][:, cols], divided[i][:])
         for half in range(2):
             cols = slice(half * T // 2, (half + 1) * T // 2)
             (nc.sync, nc.scalar)[half].dma_start(out[1][:, cols], maps[1][:, cols])

@@ -24,6 +24,8 @@ LINE = 4
 GPSIMD_COLS = 24
 ROWS = D // 32
 LIVE = P - ROWS
+FIRST_EDGES = (0, 256, 960, T)
+SPLIT = T // 2
 
 
 def tile_attend_wscat_topk_kernel(tc, qT, k_words, k_scales, offs, out):
@@ -43,10 +45,8 @@ def tile_attend_wscat_topk_kernel(tc, qT, k_words, k_scales, offs, out):
             reused.tile([P, PACK, NQ], F32, name="q_raw0", offset=64, align_bytes=64),
             keep.tile([P, PACK, NQ], F32, name="q_raw1", align_bytes=64),
         ]
-        late_words = [
-            reused.tile([P, HALF], U32, name=f"late_words{h}", offset=NQ + h * 4 * HALF, align_bytes=64)
-            for h in range(2)
-        ]
+        filler_words = keep.tile([P, NQ], U32, name="filler_words", align_bytes=64)
+        middle_words = reused.tile([P, HALF], U32, name="middle_words", offset=NQ, align_bytes=64)
         q_bf = [keep.tile([P, NQ, PACK], BF16, name=f"q_bf{b}", tag=f"q_bf{b}", align_bytes=64) for b in range(B)]
         q_words = [keep.tile([P, NQ], U32, name=f"q_words{b}", align_bytes=64) for b in range(B)]
         q_scales = [
@@ -55,10 +55,7 @@ def tile_attend_wscat_topk_kernel(tc, qT, k_words, k_scales, offs, out):
         ]
         scores = [psum.tile([P, N], F32, name=f"scores{b}") for b in range(B)]
         expd = [keep.tile([P, N], F32, name=f"expd{b}") for b in range(B)]
-        weights1 = keep.tile([P, N], F32, name="weights1")
-        maps = [keep.tile([P, T], F32, name="map0")]
-        edges = (0, 384, 768, 1408, T)
-        divided = [keep.tile([P, edges[i + 1] - edges[i]], F32, name=f"divided{i}") for i in range(len(edges) - 1)]
+        maps = [keep.tile([P, T], F32, name="map0", tag="map0")]
         neg_max = [
             keep.tile([P, 1], F32, name="neg_max0"),
             keep.tile([P, 1], F32, name="neg_max1"),
@@ -126,13 +123,16 @@ def tile_attend_wscat_topk_kernel(tc, qT, k_words, k_scales, offs, out):
             )
 
         nc.vector.tensor_copy(early_words[:], pool_words[:].indirect(listed(0, N)))
+        nc.vector.tensor_copy(filler_words[:], pool_words[:].indirect(listed(N, NQ)))
         quantize(0)
         score(0, 0, early_words[:])
-        nc.vector.tensor_copy(late_words[0][:], pool_words[:].indirect(listed(N, HALF)))
+        nc.vector.tensor_copy(middle_words[:], pool_words[:].indirect(listed(N + NQ, HALF)))
         quantize(1)
-        score(1, 0, late_words[0][:])
-        nc.vector.tensor_copy(late_words[1][:], pool_words[:].indirect(listed(N + HALF, HALF)))
-        score(1, HALF, late_words[1][:])
+        score(1, 0, filler_words[:])
+        score(1, NQ, middle_words[:])
+        last_words = keep.tile([P, NQ], U32, name="last_words", tag="q_bf1", align_bytes=64)
+        nc.vector.tensor_copy(last_words[:], pool_words[:].indirect(listed(N + NQ + HALF, NQ)))
+        score(1, NQ + HALF, last_words[:])
 
         maps.append(keep.tile([P, T], F32, name="map1", tag="pool_words", align_bytes=64))
         nc.gpsimd.memset(maps[1][:], 0.0)
@@ -146,15 +146,17 @@ def tile_attend_wscat_topk_kernel(tc, qT, k_words, k_scales, offs, out):
             )
         nc.gpsimd.tensor_tensor(inv_both[:], row_sum[:], minus_one[:], ALU.pow)
         nc.vector.tensor_copy(maps[0][:].indirect(listed(0, N)), expd[0][:])
-        nc.scalar.activation(out=weights1[:], in_=expd[1][:], func=ACT.Copy, scale=inv_sum[1])
-        nc.vector.tensor_copy(maps[1][:].indirect(listed(N, N)), weights1[:])
-        for i in range(len(divided)):
-            cols = slice(edges[i], edges[i + 1])
-            if i % 2 == 0:
-                nc.scalar.activation(out=divided[i][:], in_=maps[0][:, cols], func=ACT.Copy, scale=inv_sum[0])
-            else:
-                nc.gpsimd.tensor_scalar(divided[i][:], maps[0][:, cols], inv_sum[0], 0.0, ALU.mult, ALU.add)
-            (nc.sync if i == 1 else nc.scalar).dma_start(out[0][:, cols], divided[i][:])
+        for h in range(2):
+            nc.scalar.activation(
+                maps[1][:].indirect(listed(N + h * HALF, HALF)), expd[1][:, h * HALF : (h + 1) * HALF], ACT.Copy
+            )
+        divided = keep.tile([P, T], F32, name="divided0")
+        for first, last in zip(FIRST_EDGES, FIRST_EDGES[1:]):
+            nc.vector.tensor_scalar(divided[:, first:last], maps[0][:, first:last], inv_sum[0], None, ALU.mult)
+            nc.sync.dma_start(out[0][:, first:last], divided[:, first:last])
+        divided = keep.tile([P, T], F32, name="divided1")
+        nc.vector.tensor_scalar(divided[:, :SPLIT], maps[1][:, :SPLIT], inv_sum[1], None, ALU.mult)
+        nc.scalar.activation(out=divided[:, SPLIT:], in_=maps[1][:, SPLIT:], func=ACT.Copy, scale=inv_sum[1])
         for half in range(2):
             cols = slice(half * T // 2, (half + 1) * T // 2)
-            (nc.sync, nc.scalar)[half].dma_start(out[1][:, cols], maps[1][:, cols])
+            (nc.sync, nc.scalar)[half].dma_start(out[1][:, cols], divided[:, cols])

@@ -24,8 +24,9 @@ LINE = 4
 GPSIMD_COLS = 24
 ROWS = D // 32
 LIVE = P - ROWS
-FIRST_EDGES = (0, 256, 960, T)
+FIRST_EDGES = (0, 256, 896, T)
 SPLIT = T // 2
+AHEAD = 64
 
 
 def tile_attend_wscat_topk_kernel(tc, qT, k_words, k_scales, offs, out):
@@ -38,16 +39,16 @@ def tile_attend_wscat_topk_kernel(tc, qT, k_words, k_scales, offs, out):
         offsets = keep.tile([P, B * N // PER_COL], U16, name="offsets")
         pool_words = keep.tile([P, T], U32, name="pool_words", tag="pool_words", align_bytes=64)
         pool_scales = keep.tile([P, T], U8, name="pool_scales", align_bytes=64)
-        early_words = keep.tile([P, N], U32, name="early_words", align_bytes=64)
+        early_words = keep.tile([P, N + AHEAD], U32, name="early_words", align_bytes=64)
         key_rows = keep.tile([P, B * N], U8, name="key_rows", align_bytes=64)
         key_scales = keep.tile([P, B * N], U8, name="key_scales", align_bytes=64)
         q_raw = [
             reused.tile([P, PACK, NQ], F32, name="q_raw0", offset=64, align_bytes=64),
             keep.tile([P, PACK, NQ], F32, name="q_raw1", align_bytes=64),
         ]
-        filler_words = keep.tile([P, NQ], U32, name="filler_words", align_bytes=64)
         middle_words = reused.tile([P, HALF], U32, name="middle_words", offset=NQ, align_bytes=64)
-        q_bf = [keep.tile([P, NQ, PACK], BF16, name=f"q_bf{b}", tag=f"q_bf{b}", align_bytes=64) for b in range(B)]
+        last_words = reused.tile([P, HALF - AHEAD], U32, name="last_words", offset=NQ + 4 * HALF, align_bytes=64)
+        q_bf = [keep.tile([P, NQ, PACK], BF16, name=f"q_bf{b}", align_bytes=64) for b in range(B)]
         q_words = [keep.tile([P, NQ], U32, name=f"q_words{b}", align_bytes=64) for b in range(B)]
         q_scales = [
             keep.tile([P, NQ], U8, name="q_scales0", align_bytes=64),
@@ -122,17 +123,16 @@ def tile_attend_wscat_topk_kernel(tc, qT, k_words, k_scales, offs, out):
                 stop=True,
             )
 
-        nc.vector.tensor_copy(early_words[:], pool_words[:].indirect(listed(0, N)))
-        nc.vector.tensor_copy(filler_words[:], pool_words[:].indirect(listed(N, NQ)))
+        nc.vector.tensor_copy(early_words[:], pool_words[:].indirect(listed(0, N + AHEAD)))
         quantize(0)
-        score(0, 0, early_words[:])
-        nc.vector.tensor_copy(middle_words[:], pool_words[:].indirect(listed(N + NQ, HALF)))
+        score(0, 0, early_words[:, :N])
+        nc.vector.tensor_copy(middle_words[:], pool_words[:].indirect(listed(N + AHEAD, HALF)))
         quantize(1)
-        score(1, 0, filler_words[:])
-        score(1, NQ, middle_words[:])
-        last_words = keep.tile([P, NQ], U32, name="last_words", tag="q_bf1", align_bytes=64)
-        nc.vector.tensor_copy(last_words[:], pool_words[:].indirect(listed(N + NQ + HALF, NQ)))
-        score(1, NQ + HALF, last_words[:])
+        score(1, 0, early_words[:, N:])
+        score(1, AHEAD, middle_words[:])
+        nc.vector.tensor_copy(last_words[:], pool_words[:].indirect(listed(N + AHEAD + HALF, HALF - AHEAD)))
+        score(1, AHEAD + HALF, last_words[:, :NQ])
+        score(1, AHEAD + HALF + NQ, last_words[:, NQ:])
 
         maps.append(keep.tile([P, T], F32, name="map1", tag="pool_words", align_bytes=64))
         nc.gpsimd.memset(maps[1][:], 0.0)
@@ -153,10 +153,10 @@ def tile_attend_wscat_topk_kernel(tc, qT, k_words, k_scales, offs, out):
         divided = keep.tile([P, T], F32, name="divided0")
         for first, last in zip(FIRST_EDGES, FIRST_EDGES[1:]):
             nc.vector.tensor_scalar(divided[:, first:last], maps[0][:, first:last], inv_sum[0], None, ALU.mult)
-            nc.sync.dma_start(out[0][:, first:last], divided[:, first:last])
-        divided = keep.tile([P, T], F32, name="divided1")
-        nc.vector.tensor_scalar(divided[:, :SPLIT], maps[1][:, :SPLIT], inv_sum[1], None, ALU.mult)
-        nc.scalar.activation(out=divided[:, SPLIT:], in_=maps[1][:, SPLIT:], func=ACT.Copy, scale=inv_sum[1])
-        for half in range(2):
-            cols = slice(half * T // 2, (half + 1) * T // 2)
-            (nc.sync, nc.scalar)[half].dma_start(out[1][:, cols], divided[:, cols])
+            (nc.scalar if last == T else nc.sync).dma_start(out[0][:, first:last], divided[:, first:last])
+        low = keep.tile([P, SPLIT], F32, name="divided1_low")
+        nc.vector.tensor_scalar(low[:], maps[1][:, :SPLIT], inv_sum[1], None, ALU.mult)
+        nc.sync.dma_start(out[1][:, :SPLIT], low[:])
+        high = keep.tile([P, T - SPLIT], F32, name="divided1_high", tag="map0")
+        nc.scalar.activation(out=high[:], in_=maps[1][:, SPLIT:], func=ACT.Copy, scale=inv_sum[1])
+        nc.scalar.dma_start(out[1][:, SPLIT:], high[:])

@@ -24,9 +24,9 @@ LINE = 4
 GPSIMD_COLS = 24
 ROWS = D // 32
 LIVE = P - ROWS
-FIRST_EDGES = (0, 256, 896, T)
-SPLIT = T // 2
+MERGE_EDGES = (0, 256, 640, 1024, 1536, T)
 AHEAD = 64
+WIDE = 256
 
 
 def tile_attend_wscat_topk_kernel(tc, qT, k_words, k_scales, offs, out):
@@ -37,35 +37,31 @@ def tile_attend_wscat_topk_kernel(tc, qT, k_words, k_scales, offs, out):
         psum = ctx.enter_context(tc.psum_pool(name="psum", bufs=1))
 
         offsets = keep.tile([P, B * N // PER_COL], U16, name="offsets")
-        pool_words = keep.tile([P, T], U32, name="pool_words", tag="pool_words", align_bytes=64)
-        pool_scales = keep.tile([P, T], U8, name="pool_scales", align_bytes=64)
+        pool_words = keep.tile([P, T], U32, name="pool_words", tag="pool_words", align_bytes=WIDE)
+        pool_scales = keep.tile([P, T], U8, name="pool_scales", align_bytes=WIDE)
         early_words = keep.tile([P, N + AHEAD], U32, name="early_words", align_bytes=64)
-        key_rows = keep.tile([P, B * N], U8, name="key_rows", align_bytes=64)
-        key_scales = keep.tile([P, B * N], U8, name="key_scales", align_bytes=64)
+        key_rows = keep.tile([P, B * N], U8, name="key_rows", align_bytes=WIDE)
+        key_scales = keep.tile([P, B * N], U8, name="key_scales", align_bytes=WIDE)
         q_raw = [
-            reused.tile([P, PACK, NQ], F32, name="q_raw0", offset=64, align_bytes=64),
-            keep.tile([P, PACK, NQ], F32, name="q_raw1", align_bytes=64),
+            reused.tile([P, PACK, NQ], F32, name="q_raw0", offset=WIDE, align_bytes=WIDE),
+            keep.tile([P, PACK, NQ], F32, name="q_raw1", align_bytes=WIDE),
         ]
-        middle_words = reused.tile([P, HALF], U32, name="middle_words", offset=NQ, align_bytes=64)
-        last_words = reused.tile([P, HALF - AHEAD], U32, name="last_words", offset=NQ + 4 * HALF, align_bytes=64)
+        middle_words = reused.tile([P, HALF], U32, name="middle_words", offset=WIDE + 64, align_bytes=64)
+        last_words = reused.tile([P, HALF - AHEAD], U32, name="last_words", offset=WIDE + 64 + 4 * HALF, align_bytes=64)
         q_bf = [keep.tile([P, NQ, PACK], BF16, name=f"q_bf{b}", align_bytes=64) for b in range(B)]
         q_words = [keep.tile([P, NQ], U32, name=f"q_words{b}", align_bytes=64) for b in range(B)]
         q_scales = [
             keep.tile([P, NQ], U8, name="q_scales0", align_bytes=64),
-            reused.tile([P, NQ], U8, name="q_scales1", offset=0, align_bytes=64),
+            reused.tile([P, NQ], U8, name="q_scales1", offset=WIDE - 64, align_bytes=64),
         ]
         scores = [psum.tile([P, N], F32, name=f"scores{b}") for b in range(B)]
         expd = [keep.tile([P, N], F32, name=f"expd{b}") for b in range(B)]
-        maps = [keep.tile([P, T], F32, name="map0", tag="map0")]
-        neg_max = [
-            keep.tile([P, 1], F32, name="neg_max0"),
-            keep.tile([P, 1], F32, name="neg_max1"),
-        ]
+        raw_half = keep.tile([P, T], F32, name="raw_half")
+        neg_max = [keep.tile([P, 1], F32, name=f"neg_max{b}") for b in range(B)]
         row_sum = keep.tile([P, B], F32, name="row_sum")
-        one = keep.tile([P, B], F32, name="one")
-        minus_one = keep.tile([P, B], F32, name="minus_one")
-        inv_both = keep.tile([P, B], F32, name="inv_both")
-        inv_sum = [inv_both[:, b : b + 1] for b in range(B)]
+        one = keep.tile([P, 1], F32, name="one", tag="divided_half")
+        minus_one = keep.tile([P, 1], F32, name="minus_one")
+        inv_sum = [keep.tile([P, 1], F32, name=f"inv_sum{b}") for b in range(B)]
 
         def listed(first, count):
             return offsets[:, first // PER_COL : (first + count) // PER_COL]
@@ -76,9 +72,11 @@ def tile_attend_wscat_topk_kernel(tc, qT, k_words, k_scales, offs, out):
         for b in range(B):
             nc.sync.dma_start(q_raw[b][:], qT[b].rearrange("(p j) w -> p j w", j=PACK))
         nc.vector.memset(pool_scales[:LIVE, :].bitcast(I32), 0)
+        nc.vector.memset(raw_half[:], 0.0)
         nc.vector.memset(one[:], 1.0)
         nc.scalar.activation(out=minus_one[:], in_=one[:], func=ACT.Copy, scale=-1.0)
-        nc.vector.memset(maps[0][:], 0.0)
+        divided_half = keep.tile([P, T], F32, name="divided_half", tag="divided_half")
+        nc.gpsimd.memset(divided_half[:], 0.0)
 
         nc.vector.tensor_copy(key_rows[:], pool_scales[:].indirect(offsets[:]))
         for quad in range(4):
@@ -134,29 +132,33 @@ def tile_attend_wscat_topk_kernel(tc, qT, k_words, k_scales, offs, out):
         score(1, AHEAD + HALF, last_words[:, :NQ])
         score(1, AHEAD + HALF + NQ, last_words[:, NQ:])
 
-        maps.append(keep.tile([P, T], F32, name="map1", tag="pool_words", align_bytes=64))
-        nc.gpsimd.memset(maps[1][:], 0.0)
+        map1 = keep.tile([P, T], F32, name="map1", tag="pool_words", align_bytes=WIDE)
+        nc.gpsimd.memset(map1[:], 0.0)
 
         for b in range(B):
             nc.vector.tensor_reduce(out=neg_max[b][:], in_=scores[b][:], axis=AXIS.X, op=ALU.max, negate=True)
-
         for b in range(B):
             nc.scalar.activation(
                 out=expd[b][:], in_=scores[b][:], func=ACT.Exp, bias=neg_max[b][:], accum_out=row_sum[:, b : b + 1]
             )
-        nc.gpsimd.tensor_tensor(inv_both[:], row_sum[:], minus_one[:], ALU.pow)
-        nc.vector.tensor_copy(maps[0][:].indirect(listed(0, N)), expd[0][:])
-        for h in range(2):
-            nc.scalar.activation(
-                maps[1][:].indirect(listed(N + h * HALF, HALF)), expd[1][:, h * HALF : (h + 1) * HALF], ACT.Copy
+        nc.vector.reciprocal(inv_sum[0][:], row_sum[:, 0:1])
+        nc.gpsimd.tensor_tensor(inv_sum[1][:], row_sum[:, 1:2], minus_one[:], ALU.pow)
+
+        nc.vector.tensor_copy(raw_half[:].indirect(listed(HALF, HALF)), expd[0][:, HALF:])
+        nc.scalar.activation(
+            divided_half[:].indirect(listed(0, HALF)), expd[0][:, :HALF], ACT.Copy, scale=inv_sum[0][:]
+        )
+        nc.scalar.activation(map1[:].indirect(listed(N, N)), expd[1][:], ACT.Copy, scale=inv_sum[1][:])
+
+        map0 = keep.tile([P, T], F32, name="map0", align_bytes=WIDE)
+        for first, last in zip(MERGE_EDGES, MERGE_EDGES[1:]):
+            nc.vector.scalar_tensor_tensor(
+                map0[:, first:last],
+                raw_half[:, first:last],
+                inv_sum[0][:],
+                divided_half[:, first:last],
+                ALU.mult,
+                ALU.add,
             )
-        divided = keep.tile([P, T], F32, name="divided0")
-        for first, last in zip(FIRST_EDGES, FIRST_EDGES[1:]):
-            nc.vector.tensor_scalar(divided[:, first:last], maps[0][:, first:last], inv_sum[0], None, ALU.mult)
-            (nc.scalar if last == T else nc.sync).dma_start(out[0][:, first:last], divided[:, first:last])
-        low = keep.tile([P, SPLIT], F32, name="divided1_low")
-        nc.vector.tensor_scalar(low[:], maps[1][:, :SPLIT], inv_sum[1], None, ALU.mult)
-        nc.sync.dma_start(out[1][:, :SPLIT], low[:])
-        high = keep.tile([P, T - SPLIT], F32, name="divided1_high", tag="map0")
-        nc.scalar.activation(out=high[:], in_=maps[1][:, SPLIT:], func=ACT.Copy, scale=inv_sum[1])
-        nc.scalar.dma_start(out[1][:, SPLIT:], high[:])
+            nc.sync.dma_start(out[0][:, first:last], map0[:, first:last])
+        nc.scalar.dma_start(out[1], map1[:])

@@ -160,5 +160,6 @@ def tile_attend_wscat_topk_kernel(tc, qT, k_words, k_scales, offs, out):
                 ALU.mult,
                 ALU.add,
             )
-            nc.sync.dma_start(out[0][:, first:last], map0[:, first:last])
-        nc.scalar.dma_start(out[1], map1[:])
+            nc.scalar.dma_start(out[0][:, first:last], map0[:, first:last])
+        nc.sync.dma_start(out[1][:, : T // 2], map1[:, : T // 2])
+        nc.scalar.dma_start(out[1][:, T // 2 :], map1[:, T // 2 :])

@@ -25,7 +25,7 @@ GPSIMD_COLS = 24
 ROWS = D // 32
 LIVE = P - ROWS
 MERGE_EDGES = (0, 256, 640, 1024, 1536, T)
-AHEAD = 64
+AHEAD = 128
 WIDE = 256
 
 
@@ -129,8 +129,7 @@ def tile_attend_wscat_topk_kernel(tc, qT, k_words, k_scales, offs, out):
         score(1, 0, early_words[:, N:])
         score(1, AHEAD, middle_words[:])
         nc.vector.tensor_copy(last_words[:], pool_words[:].indirect(listed(N + AHEAD + HALF, HALF - AHEAD)))
-        score(1, AHEAD + HALF, last_words[:, :NQ])
-        score(1, AHEAD + HALF + NQ, last_words[:, NQ:])
+        score(1, AHEAD + HALF, last_words[:])
 
         map1 = keep.tile([P, T], F32, name="map1", tag="pool_words", align_bytes=WIDE)
         nc.gpsimd.memset(map1[:], 0.0)

@@ -21,7 +21,7 @@ PACK = 4
 HALF = N // 2
 PER_COL = 16
 LINE = 4
-GPSIMD_COLS = 24
+GPSIMD_COLS = 40
 ROWS = D // 32
 LIVE = P - ROWS
 MERGE_EDGES = (0, 256, 640, 1024, 1536, T)

from contextlib import ExitStack

import concourse.mybir as mybir

B, N, T, D, NQ = 2, 512, 2048, 512, 128
FLOPS = 2 * B * NQ * N * D

F32 = mybir.dt.float32
BF16 = mybir.dt.bfloat16
I32 = mybir.dt.int32
U32 = mybir.dt.uint32
U16 = mybir.dt.uint16
U8 = mybir.dt.uint8
FP8X4 = mybir.dt.float8_e4m3fn_x4
ACT = mybir.ActivationFunctionType
ALU = mybir.AluOpType
AXIS = mybir.AxisListType

P = 128
PACK = 4
HALF = N // 2
PER_COL = 16
LINE = 4
GPSIMD_COLS = 40
ROWS = D // 32
LIVE = P - ROWS
MERGE_EDGES = (0, 256, 640, 1024, 1536, T)
AHEAD = 128
WIDE = 256


def tile_attend_wscat_topk_kernel(tc, qT, k_words, k_scales, offs, out):
    nc = tc.nc
    with ExitStack() as ctx:
        keep = ctx.enter_context(tc.tile_pool(name="keep", bufs=1))
        reused = ctx.enter_context(tc.tile_pool(name="reused", bufs=1))
        psum = ctx.enter_context(tc.psum_pool(name="psum", bufs=1))

        offsets = keep.tile([P, B * N // PER_COL], U16, name="offsets")
        pool_words = keep.tile([P, T], U32, name="pool_words", tag="pool_words", align_bytes=WIDE)
        pool_scales = keep.tile([P, T], U8, name="pool_scales", align_bytes=WIDE)
        early_words = keep.tile([P, N + AHEAD], U32, name="early_words", align_bytes=64)
        key_rows = keep.tile([P, B * N], U8, name="key_rows", align_bytes=WIDE)
        key_scales = keep.tile([P, B * N], U8, name="key_scales", align_bytes=WIDE)
        q_raw = [
            reused.tile([P, PACK, NQ], F32, name="q_raw0", offset=WIDE, align_bytes=WIDE),
            keep.tile([P, PACK, NQ], F32, name="q_raw1", align_bytes=WIDE),
        ]
        middle_words = reused.tile([P, HALF], U32, name="middle_words", offset=WIDE + 64, align_bytes=64)
        last_words = reused.tile([P, HALF - AHEAD], U32, name="last_words", offset=WIDE + 64 + 4 * HALF, align_bytes=64)
        q_bf = [keep.tile([P, NQ, PACK], BF16, name=f"q_bf{b}", align_bytes=64) for b in range(B)]
        q_words = [keep.tile([P, NQ], U32, name=f"q_words{b}", align_bytes=64) for b in range(B)]
        q_scales = [
            keep.tile([P, NQ], U8, name="q_scales0", align_bytes=64),
            reused.tile([P, NQ], U8, name="q_scales1", offset=WIDE - 64, align_bytes=64),
        ]
        scores = [psum.tile([P, N], F32, name=f"scores{b}") for b in range(B)]
        expd = [keep.tile([P, N], F32, name=f"expd{b}") for b in range(B)]
        raw_half = keep.tile([P, T], F32, name="raw_half")
        neg_max = [keep.tile([P, 1], F32, name=f"neg_max{b}") for b in range(B)]
        row_sum = keep.tile([P, B], F32, name="row_sum")
        one = keep.tile([P, 1], F32, name="one", tag="divided_half")
        minus_one = keep.tile([P, 1], F32, name="minus_one")
        inv_sum = [keep.tile([P, 1], F32, name=f"inv_sum{b}") for b in range(B)]

        def listed(first, count):
            return offsets[:, first // PER_COL : (first + count) // PER_COL]

        nc.sync.dma_start(pool_scales[LIVE:, :].bitcast(I32), k_scales[0].bitcast(I32))
        nc.sync.dma_start(offsets[:], offs)
        nc.sync.dma_start(pool_words[:].bitcast(I32), k_words[0].rearrange("p t r -> p (t r)").bitcast(I32))
        for b in range(B):
            nc.sync.dma_start(q_raw[b][:], qT[b].rearrange("(p j) w -> p j w", j=PACK))
        nc.vector.memset(pool_scales[:LIVE, :].bitcast(I32), 0)
        nc.vector.memset(raw_half[:], 0.0)
        nc.vector.memset(one[:], 1.0)
        nc.scalar.activation(out=minus_one[:], in_=one[:], func=ACT.Copy, scale=-1.0)
        divided_half = keep.tile([P, T], F32, name="divided_half", tag="divided_half")
        nc.gpsimd.memset(divided_half[:], 0.0)

        nc.vector.tensor_copy(key_rows[:], pool_scales[:].indirect(offsets[:]))
        for quad in range(4):
            nc.sync.dma_start(
                key_scales[32 * quad : 32 * quad + 4, :].bitcast(I32),
                key_rows[LIVE + 4 * quad : LIVE + 4 * quad + 4, :].bitcast(I32),
            )

        def walk(b, cols):
            return (
                q_bf[b][:, cols, :].rearrange("p (c i) j -> p c j i", i=LINE),
                q_raw[b][:, :, cols].rearrange("p j (c i) -> p c j i", i=LINE),
            )

        def quantize(b):
            shared = GPSIMD_COLS if b == 0 else 0
            nc.scalar.copy(*walk(b, slice(0, NQ - shared)))
            if shared:
                nc.gpsimd.tensor_scalar(
                    q_bf[b][:, NQ - shared :, :],
                    q_raw[b][:, :, NQ - shared :].rearrange("p j w -> p w j"),
                    1.0,
                    0.0,
                    ALU.mult,
                    ALU.add,
                )
            nc.vector.quantize_mx(
                out=q_words[b][:].bitcast(FP8X4),
                scales=q_scales[b][:],
                in_=q_bf[b][:].rearrange("p w j -> p (w j)"),
            )

        def score(b, first, words):
            count = words.shape[1]
            nc.tensor.matmul_mx(
                out=scores[b][:, first : first + count],
                lhsT=q_words[b][:].bitcast(FP8X4),
                lhsT_scale=q_scales[b][:],
                rhs=words.bitcast(FP8X4),
                rhs_scale=key_scales[:, b * N + first : b * N + first + count],
                start=True,
                stop=True,
            )

        nc.vector.tensor_copy(early_words[:], pool_words[:].indirect(listed(0, N + AHEAD)))
        quantize(0)
        score(0, 0, early_words[:, :N])
        nc.vector.tensor_copy(middle_words[:], pool_words[:].indirect(listed(N + AHEAD, HALF)))
        quantize(1)
        score(1, 0, early_words[:, N:])
        score(1, AHEAD, middle_words[:])
        nc.vector.tensor_copy(last_words[:], pool_words[:].indirect(listed(N + AHEAD + HALF, HALF - AHEAD)))
        score(1, AHEAD + HALF, last_words[:])

        map1 = keep.tile([P, T], F32, name="map1", tag="pool_words", align_bytes=WIDE)
        nc.gpsimd.memset(map1[:], 0.0)

        for b in range(B):
            nc.vector.tensor_reduce(out=neg_max[b][:], in_=scores[b][:], axis=AXIS.X, op=ALU.max, negate=True)
        for b in range(B):
            nc.scalar.activation(
                out=expd[b][:], in_=scores[b][:], func=ACT.Exp, bias=neg_max[b][:], accum_out=row_sum[:, b : b + 1]
            )
        nc.vector.reciprocal(inv_sum[0][:], row_sum[:, 0:1])
        nc.gpsimd.tensor_tensor(inv_sum[1][:], row_sum[:, 1:2], minus_one[:], ALU.pow)

        nc.vector.tensor_copy(raw_half[:].indirect(listed(HALF, HALF)), expd[0][:, HALF:])
        nc.scalar.activation(
            divided_half[:].indirect(listed(0, HALF)), expd[0][:, :HALF], ACT.Copy, scale=inv_sum[0][:]
        )
        nc.scalar.activation(map1[:].indirect(listed(N, N)), expd[1][:], ACT.Copy, scale=inv_sum[1][:])

        map0 = keep.tile([P, T], F32, name="map0", align_bytes=WIDE)
        for first, last in zip(MERGE_EDGES, MERGE_EDGES[1:]):
            nc.vector.scalar_tensor_tensor(
                map0[:, first:last],
                raw_half[:, first:last],
                inv_sum[0][:],
                divided_half[:, first:last],
                ALU.mult,
                ALU.add,
            )
            nc.scalar.dma_start(out[0][:, first:last], map0[:, first:last])
        nc.sync.dma_start(out[1][:, : T // 2], map1[:, : T // 2])
        nc.scalar.dma_start(out[1][:, T // 2 :], map1[:, T // 2 :])
